import numpy as np
import ml_dtypes


def mxq(x, axis, fmt="e4m3"):
    dtype, down = {"e4m3": (ml_dtypes.float8_e4m3fn, 7), "e5m2": (ml_dtypes.float8_e5m2, 14)}[fmt]
    v = np.moveaxis(np.asarray(x, np.float32).astype(ml_dtypes.bfloat16).astype(np.float64), axis, -1)
    blocks = v.reshape(v.shape[:-1] + (-1, 32))
    amax = np.abs(blocks).max(-1, keepdims=True)
    byte = np.maximum(np.where(amax > 0, np.frexp(amax)[1] - 1 + 127, 0) - down, 1)
    scale = np.exp2(byte - 127.0)
    codes = (blocks / scale).astype(np.float32).astype(dtype).astype(np.float64)
    return np.moveaxis((codes * scale).reshape(v.shape), -1, axis)


WIDE = False


def mx_kscale(k):
    if not WIDE:
        return np.ones(k)
    levels = np.array([10, -10, 5, -5, 0])
    if k % 512:
        return np.exp2(np.random.permutation(np.resize(levels, k // 32))).repeat(32)
    a = np.empty((k // 512, 16))
    for p in range(k // 512):
        a[p, :8] = np.random.permutation(np.resize(levels, 8))
        for g in range(8):
            far = levels[np.abs(levels - a[p, g]) >= 10]
            a[p, g + 8] = far[np.random.randint(len(far))]
    return np.exp2(a.ravel()).repeat(32)


def f64(x):
    return np.asarray(x).astype(np.float64)


E2M1 = np.array([0.0, 0.5, 1.0, 1.5, 2.0, 3.0, 4.0, 6.0, -0.0, -0.5, -1.0, -1.5, -2.0, -3.0, -4.0, -6.0])


def pack_weight(w, fmt):
    k, n = w.shape
    w = f64(np.asarray(w, np.float32).astype(ml_dtypes.bfloat16)).reshape(k // 32, 32, n)
    amax = np.abs(w).max(1)
    if fmt == "e4m3":
        byte = np.frexp(amax)[1] - 1 + 127 - 7
    else:
        mant, ex = np.frexp(amax / 6.0)
        byte = np.where(mant > 0.5, ex, ex - 1) + 127
    byte = np.clip(np.where(amax > 0, byte, 1), 1, 254)
    scaled = (w * np.exp2(127.0 - byte)[:, None, :]).reshape(k, n).astype(np.float32)
    by_word = np.ascontiguousarray(scaled.reshape(k // 512, 128, 4, n).transpose(0, 1, 3, 2))
    if fmt == "e4m3":
        words = by_word.astype(ml_dtypes.float8_e4m3fn).view(np.uint8)
    else:
        c = by_word.astype(ml_dtypes.float4_e2m1fn).view(np.uint8) & 0xF
        words = (c[..., 0::2] | (c[..., 1::2] << 4)).reshape(k // 512, 128, 2 * n)
    return np.ascontiguousarray(words), np.ascontiguousarray(byte.astype(np.uint8).reshape(k // 512, 16, n))


def unpack_weight(words, scales, fmt):
    g, _, n = scales.shape
    words = np.ascontiguousarray(words).reshape(g, 128, n, -1)
    if fmt == "e4m3":
        vals = words.view(ml_dtypes.float8_e4m3fn).astype(np.float64)
    else:
        nib = np.empty((g, 128, n, 4), np.uint8)
        nib[..., 0::2] = words & 0xF
        nib[..., 1::2] = words >> 4
        vals = E2M1[nib]
    vals = vals * np.repeat(np.exp2(scales.astype(np.float64) - 127.0), 8, axis=1)[..., None]
    return vals.transpose(0, 1, 3, 2).reshape(g * 512, n)


K, L, T, R, N = 1024, 512, 512, 512, 512


def setup_inputs():
    n = np.random.standard_normal
    fk = mx_kscale(K)
    fl = mx_kscale(L)
    fr = mx_kscale(R)
    xtp = pack_weight(n((K, T)) * np.random.uniform(0.3, 1.7, (1, T)) / fk[:, None], "e4m3")
    wap = pack_weight(n((K, R)) * 1 / np.sqrt(K) * fk[:, None], "e2m1")
    xqp = pack_weight(n((L, T)) * 0.5 / fl[:, None], "e2m1")
    wcp = pack_weight(n((L, R)) * 1 / np.sqrt(L) * fl[:, None], "e4m3")
    wbp = pack_weight(n((R, N)) * 1 / np.sqrt(R) / fr[:, None], "e2m1")
    wyp = pack_weight(n((K, N)) * 1 / np.sqrt(K) * fk[:, None], "e4m3")
    return {
        "xt_words": xtp[0],
        "xt_scales": xtp[1],
        "wa_words": wap[0],
        "wa_scales": wap[1],
        "xq_words": xqp[0],
        "xq_scales": xqp[1],
        "wc_words": wcp[0],
        "wc_scales": wcp[1],
        "fr": (np.random.uniform(0.5, 2.0, (R, 1)) * fr[:, None]).astype(np.float32),
        "wb_words": wbp[0],
        "wb_scales": wbp[1],
        "wy_words": wyp[0],
        "wy_scales": wyp[1],
    }


def reference(xt_words, xt_scales, wa_words, wa_scales, xq_words, xq_scales, wc_words, wc_scales, fr, wb_words, wb_scales, wy_words, wy_scales):
    xtu = unpack_weight(xt_words, xt_scales, "e4m3")
    wau = unpack_weight(wa_words, wa_scales, "e2m1")
    xqu = unpack_weight(xq_words, xq_scales, "e2m1")
    wcu = unpack_weight(wc_words, wc_scales, "e4m3")
    wbu = unpack_weight(wb_words, wb_scales, "e2m1")
    wyu = unpack_weight(wy_words, wy_scales, "e4m3")
    z = xtu.T @ wau + xqu.T @ wcu
    d = z - np.mean(z, axis=1, keepdims=True)
    e = d / np.sqrt(np.mean(np.square(d), axis=1, keepdims=True) + 0.01)
    et = e.T
    hid = et * f64(fr)
    hidq = mxq(hid, 0, "e4m3")
    y = wbu.T @ hidq + wyu.T @ xtu
    return y

@@ -1,0 +1,229 @@
+from contextlib import ExitStack
+
+import concourse.mybir as mybir
+from concourse.masks import make_identity
+
+K, L, T, R, N = 1024, 512, 512, 512, 512
+FLOPS = 2 * T * R * (K + L) + 2 * N * T * (R + K)
+
+F32 = mybir.dt.float32
+BF16 = mybir.dt.bfloat16
+I32 = mybir.dt.int32
+U32 = mybir.dt.uint32
+U8 = mybir.dt.uint8
+E4M3 = mybir.dt.float8_e4m3fn_x4
+E2M1 = mybir.dt.float4_e2m1fn_x4
+ACT = mybir.ActivationFunctionType
+ALU = mybir.AluOpType
+
+P = 128
+W = 512
+TILES = 4
+EPS = 0.01
+
+
+def tile_mix_hidden_rows_levelled_kernel(
+    tc, xt_words, xt_scales, wa_words, wa_scales, xq_words, xq_scales, wc_words, wc_scales,
+    fr, wb_words, wb_scales, wy_words, wy_scales, out,
+):
+    nc = tc.nc
+    with ExitStack() as ctx:
+        sb = ctx.enter_context(tc.tile_pool(name="sb", bufs=1))
+        ps = ctx.enter_context(tc.psum_pool(name="ps", bufs=1))
+        ctx.enter_context(tc.manual_schedule())
+
+        def plane(name, passes, eng):
+            t = sb.tile([P, passes * W], U8, name=name, align_bytes=64)
+            eng.memset(t[:].bitcast(I32), 0)
+            return t
+
+        def load_scale_row(eng, t, scales, r):
+            passes = scales.shape[0]
+            eng.dma_start(
+                out=t[r:P:32, :].bitcast(I32).rearrange("q (z c) -> q z c", z=passes),
+                in_=scales.bitcast(I32).rearrange("z (q r) c -> r q z c", r=4)[r],
+            )
+
+        def load_words(eng, name, src):
+            t = sb.tile([P, src.shape[1]], U8, name=name, align_bytes=64)
+            eng.dma_start(out=t[:].bitcast(I32), in_=src.bitcast(I32))
+            return t
+
+        def fp8(w, z):
+            return w[z].rearrange("p n j -> p (n j)")
+
+        ident = sb.tile([P, P], F32, name="ident")
+        make_identity(nc, ident[:])
+        xt_s = plane("xt_s", 2, nc.vector)
+        wa_s = plane("wa_s", 2, nc.vector)
+        wc_s = plane("wc_s", 1, nc.vector)
+        xq_s = plane("xq_s", 1, nc.vector)
+        wy_s = plane("wy_s", 2, nc.vector)
+        wb_s = plane("wb_s", 1, nc.vector)
+        warm = sb.tile([P, 1], F32, name="warm")
+        nc.vector.memset(warm[:], 1.0)
+
+        for r in range(4):
+            load_scale_row(nc.sync, xt_s, xt_scales, r)
+            load_scale_row(nc.scalar, wa_s, wa_scales, r)
+        warm2 = sb.tile([P, 1], F32, name="warm2")
+        nc.scalar.activation(out=warm2[:], in_=warm[:], func=ACT.Abs_reciprocal_sqrt, bias=EPS)
+        fr_col = sb.tile([P, 4], F32, name="fr_col")
+        nc.sync.dma_start(out=fr_col[:], in_=fr.rearrange("(p j) o -> p (j o)", j=4))
+        xt = []
+        wa = []
+        for g in range(2):
+            xt.append(load_words(nc.sync, "xt%d" % g, fp8(xt_words, g)))
+            wa.append(load_words(nc.sync, "wa%d" % g, wa_words[g]))
+        xq = load_words(nc.sync, "xq", xq_words[0])
+        wc = load_words(nc.sync, "wc", fp8(wc_words, 0))
+        for r in range(4):
+            load_scale_row(nc.sync, xq_s, xq_scales, r)
+        for r in range(4):
+            load_scale_row(nc.gpsimd, wc_s, wc_scales, r)
+        wy = [load_words(nc.sync, "wy%d" % z, fp8(wy_words, z)) for z in range(2)]
+        for r in range(4):
+            load_scale_row(nc.sync, wy_s, wy_scales, r)
+        wb = load_words(nc.sync, "wb", wb_words[0])
+        for r in range(4):
+            load_scale_row(nc.gpsimd, wb_s, wb_scales, r)
+
+        fr_ps = ps.tile([P, 4, P], F32, name="fr_ps", tag="o3")
+        for j in range(4):
+            nc.tensor.transpose(fr_ps[:, j, :], fr_col[:, j:j + 1].to_broadcast([P, P]), ident[:])
+        fr_row = sb.tile([P, W], F32, name="fr_row")
+        nc.vector.tensor_copy(out=fr_row[:].rearrange("m (p j) -> m p j", j=4), in_=fr_ps[:].rearrange("m j p -> m p j"))
+
+        z = [ps.tile([P, W], F32, name="z%d" % i, tag="z%d" % i) for i in range(TILES)]
+        stats = [None] * TILES
+        mv = [None] * TILES
+        rstd = [None] * TILES
+        cen = [None] * TILES
+        hid = [None] * TILES
+        turned = [None] * TILES
+        grouped = [None] * TILES
+        codes = [None] * TILES
+        hsc = [None] * TILES
+
+        def cols(i, width=1):
+            return slice(i * P * width, (i + 1) * P * width)
+
+        def first_layer(i, g):
+            if g < 2:
+                nc.tensor.matmul_mx(
+                    out=z[i][:], lhsT=xt[g][:, cols(i, 4)].bitcast(E4M3), lhsT_scale=xt_s[:, g * W + i * P:g * W + (i + 1) * P],
+                    rhs=wa[g][:].bitcast(E2M1), rhs_scale=wa_s[:, g * W:(g + 1) * W], start=(g == 0), stop=False)
+            else:
+                nc.tensor.matmul_mx(
+                    out=z[i][:], lhsT=xq[:, cols(i, 2)].bitcast(E2M1), lhsT_scale=xq_s[:, cols(i)],
+                    rhs=wc[:].bitcast(E4M3), rhs_scale=wc_s[:], start=False, stop=True)
+
+        def row_stats(i):
+            stats[i] = sb.tile([P, 6], F32, name="stats%d" % i)
+            mv[i] = sb.tile([P, 2], F32, name="mv%d" % i)
+            rstd[i] = sb.tile([P, 1], F32, name="rstd%d" % i)
+            nc.vector.bn_stats(out=stats[i][:], in_=z[i][:])
+            nc.vector.bn_aggr(out=mv[i][:], in_=stats[i][:])
+            nc.scalar.activation(out=rstd[i][:], in_=mv[i][:, 1:2], func=ACT.Abs_reciprocal_sqrt, bias=EPS)
+
+        def centre(i):
+            cen[i] = sb.tile([P, W], F32, name="cen%d" % i)
+            nc.vector.scalar_tensor_tensor(out=cen[i][:], in0=z[i][:], scalar=mv[i][:, 0:1], in1=fr_row[:],
+                                           op0=ALU.subtract, op1=ALU.mult)
+
+        def level(i):
+            hid[i] = sb.tile([P, W], BF16, name="hid%d" % i)
+            nc.scalar.activation(out=hid[i][:].rearrange("t (u p e) -> t u p e", u=2, e=2),
+                                 in_=cen[i][:].rearrange("t (p u e) -> t u p e", u=2, e=2),
+                                 func=ACT.Copy, scale=rstd[i][:])
+
+        def turn(i):
+            turned[i] = ps.tile([P, 2, P], F32, name="turned%d" % i, tag="z%d" % i)
+            for u in range(2):
+                nc.tensor.transpose(turned[i][:, u, :], hid[i][:].bitcast(F32)[:, cols(u)], ident[:])
+
+        def gather(i):
+            grouped[i] = sb.tile([P, W], BF16, name="grouped%d" % i, align_bytes=64)
+            nc.scalar.copy(out=grouped[i][:].bitcast(F32).rearrange("p (t u) -> p t u", u=2),
+                           in_=turned[i][:].rearrange("p u t -> p t u"))
+
+        def quantise(i):
+            codes[i] = sb.tile([P, P], U32, name="codes%d" % i, align_bytes=64)
+            hsc[i] = sb.tile([P, P], U8, name="hsc%d" % i, align_bytes=64)
+            nc.vector.quantize_mx(out=codes[i][:].bitcast(E4M3), scales=hsc[i][:], in_=grouped[i][:])
+
+        banks = [(0, 256, 0, 2, "o0"), (0, 256, 2, 2, "o1"), (256, 128, 0, 4, "o2"), (384, 128, 0, 2, "o3"), (384, 128, 2, 2, "z0")]
+        y = [None] * len(banks)
+
+        def skip(b):
+            t0, nt, a0, na, tag = banks[b]
+            y[b] = ps.tile([P, na, nt], F32, name="y%d" % b, tag=tag)
+            for a in range(a0, a0 + na):
+                for g in range(2):
+                    nc.tensor.matmul_mx(
+                        out=y[b][:, a - a0, :], lhsT=wy[g][:, cols(a, 4)].bitcast(E4M3),
+                        lhsT_scale=wy_s[:, g * W + a * P:g * W + (a + 1) * P],
+                        rhs=xt[g][:, 4 * t0:4 * (t0 + nt)].bitcast(E4M3), rhs_scale=xt_s[:, g * W + t0:g * W + t0 + nt],
+                        start=(a == a0 and g == 0), stop=False)
+
+        def second_layer(i):
+            for b, (t0, nt, a0, na, tag) in enumerate(banks):
+                if t0 <= i * P < t0 + nt:
+                    for a in range(a0, a0 + na):
+                        nc.tensor.matmul_mx(
+                            out=y[b][:, a - a0, i * P - t0:(i + 1) * P - t0], lhsT=wb[:, cols(a, 2)].bitcast(E2M1),
+                            lhsT_scale=wb_s[:, cols(a)], rhs=codes[i][:].bitcast(E4M3), rhs_scale=hsc[i][:],
+                            start=False, stop=(a == a0 + na - 1 and (i + 1) * P == t0 + nt))
+
+        def store(b, eng, queue):
+            t0, nt, a0, na, tag = banks[b]
+            res = sb.tile([P, na, nt], F32, name="res%d" % b)
+            if eng == "s":
+                nc.scalar.copy(out=res[:], in_=y[b][:])
+            else:
+                nc.vector.tensor_copy(out=res[:], in_=y[b][:])
+            queue.dma_start(out=out.rearrange("(a p) t -> p a t", p=P)[:, a0:a0 + na, t0:t0 + nt], in_=res[:])
+
+        for i, g in [(0, 0), (1, 0), (0, 1), (0, 2), (1, 1), (1, 2)]:
+            first_layer(i, g)
+        for i in range(2, 4):
+            for g in range(3):
+                first_layer(i, g)
+        row_stats(0)
+        centre(0)
+        level(0)
+        turn(0)
+        row_stats(1)
+        centre(1)
+        level(1)
+        gather(0)
+        skip(0)
+        skip(1)
+        turn(1)
+        row_stats(2)
+        quantise(0)
+        centre(2)
+        level(2)
+        gather(1)
+        second_layer(0)
+        skip(2)
+        turn(2)
+        row_stats(3)
+        quantise(1)
+        centre(3)
+        level(3)
+        gather(2)
+        second_layer(1)
+        turn(3)
+        gather(3)
+        store(0, "v", nc.sync)
+        quantise(2)
+        quantise(3)
+        skip(3)
+        skip(4)
+        second_layer(2)
+        second_layer(3)
+        store(1, "s", nc.sync)
+        store(2, "v", nc.sync)
+        store(4, "s", nc.scalar)
+        store(3, "v", nc.sync)

@@ -17,9 +17,19 @@ ACT = mybir.ActivationFunctionType
 ALU = mybir.AluOpType
 
 P = 128
-W = 512
-TILES = 4
+PACK = 4
+COLS = 512
+TILES = T // P
+FEATURE_TILES = N // P
+K_PASSES = K // (P * PACK)
+E4M3_BYTES = 4
+E2M1_BYTES = 2
+QUADRANT = 32
 EPS = 0.01
+
+
+def span(i, width):
+    return slice(i * width, (i + 1) * width)
 
 
 def tile_mix_hidden_rows_levelled_kernel(
@@ -32,198 +42,228 @@ def tile_mix_hidden_rows_levelled_kernel(
         ps = ctx.enter_context(tc.psum_pool(name="ps", bufs=1))
         ctx.enter_context(tc.manual_schedule())
 
-        def plane(name, passes, eng):
-            t = sb.tile([P, passes * W], U8, name=name, align_bytes=64)
-            eng.memset(t[:].bitcast(I32), 0)
-            return t
 
-        def load_scale_row(eng, t, scales, r):
+        def zeroed_plane(name, passes, engine):
+            plane = sb.tile([P, passes * COLS], U8, name=name, align_bytes=64)
+            engine.memset(plane[:].bitcast(I32), 0)
+            return plane
+
+        def load_scale_rows(queue, plane, scales, rows):
             passes = scales.shape[0]
-            eng.dma_start(
-                out=t[r:P:32, :].bitcast(I32).rearrange("q (z c) -> q z c", z=passes),
-                in_=scales.bitcast(I32).rearrange("z (q r) c -> r q z c", r=4)[r],
+            by_r = scales.bitcast(I32).rearrange("g (q r) c -> r q g c", r=4)
+            for r in rows:
+                queue.dma_start(
+                    out=plane[r:P:QUADRANT, :].bitcast(I32).rearrange("q (g c) -> q g c", g=passes), in_=by_r[r]
+                )
+
+        def load_words(name, words):
+            passes, width = words.shape[0], words.shape[2]
+            packed = sb.tile([P, passes * width], U8, name=name, align_bytes=64)
+            nc.sync.dma_start(
+                out=packed[:].bitcast(I32).rearrange("p (g c) -> p g c", g=passes),
+                in_=words.bitcast(I32).rearrange("g p c -> p g c"),
+            )
+            return [packed[:, span(g, width)] for g in range(passes)]
+
+        def merged(words):
+            return words.rearrange("g p c j -> g p (c j)")
+
+        xt_plane = zeroed_plane("xt_plane", K_PASSES, nc.gpsimd)
+        wa_plane = zeroed_plane("wa_plane", K_PASSES, nc.vector)
+        wc_plane = zeroed_plane("wc_plane", 1, nc.vector)
+        xq_plane = zeroed_plane("xq_plane", 1, nc.vector)
+        wy_plane = zeroed_plane("wy_plane", K_PASSES, nc.vector)
+        wb_plane = zeroed_plane("wb_plane", 1, nc.vector)
+
+        vector_tile = 1
+        moments = [sb.tile([P, 3], F32, name="moments%d" % i) for i in range(TILES)]
+        for i in range(TILES):
+            if i != vector_tile:
+                nc.vector.memset(moments[i][:, 0:1], -1.0)
+
+        half_bytes = 2 * P * E4M3_BYTES
+        wa = load_words("wa", wa_words)
+        load_scale_rows(nc.scalar, xt_plane, xt_scales, range(4))
+        table_preload = sb.tile([P, 1], F32, name="table_preload")
+        nc.scalar.activation(out=table_preload[:], in_=moments[0][:, 0:1], func=ACT.Abs_reciprocal_sqrt, bias=EPS)
+        load_scale_rows(nc.sync, wa_plane, wa_scales, (0, 1))
+        xt_halves = [load_words("xt_half0", merged(xt_words)[:, :, span(0, half_bytes)])]
+        load_scale_rows(nc.sync, wa_plane, wa_scales, (2, 3))
+        load_scale_rows(nc.sync, xq_plane, xq_scales, (0,))
+        wc = load_words("wc", merged(wc_words))[0]
+        load_scale_rows(nc.sync, xq_plane, xq_scales, (1, 2, 3))
+        xq = load_words("xq", xq_words)[0]
+        load_scale_rows(nc.sync, wc_plane, wc_scales, (0, 1))
+        load_scale_rows(nc.gpsimd, wc_plane, wc_scales, (2, 3))
+        xt_halves.append(load_words("xt_half1", merged(xt_words)[:, :, span(1, half_bytes)]))
+        wy = load_words("wy", merged(wy_words))
+        load_scale_rows(nc.sync, wy_plane, wy_scales, range(4))
+        wb = load_words("wb", wb_words)[0]
+        load_scale_rows(nc.sync, wb_plane, wb_scales, range(4))
+
+        identity = sb.tile([P, P], F32, name="identity")
+        make_identity(nc, identity[:])
+        fr_pos = sb.tile([P, PACK], F32, name="fr_pos")
+        nc.gpsimd.dma_start(out=fr_pos[:], in_=fr.rearrange("(p j) o -> p (j o)", j=PACK))
+        fr_neg = sb.tile([P, PACK], F32, name="fr_neg")
+        nc.gpsimd.tensor_scalar(out=fr_neg[:], in0=fr_pos[:], scalar1=-1.0, scalar2=0.0, op0=ALU.mult, op1=ALU.add)
+
+        def xt_tile(i, g):
+            codes = xt_halves[i // 2][g][:, span(i % 2, P * E4M3_BYTES)].bitcast(E4M3)
+            return codes, xt_plane[:, span(g * TILES + i, P)]
+
+
+        z = [ps.tile([P, R], F32, name="z%d" % i, tag="hidden%d" % i) for i in range(TILES)]
+
+        def xt_wa_pass(i, g):
+            codes, scales = xt_tile(i, g)
+            nc.tensor.matmul_mx(
+                out=z[i][:], lhsT=codes, lhsT_scale=scales,
+                rhs=wa[g].bitcast(E2M1), rhs_scale=wa_plane[:, span(g, COLS)], start=(g == 0), stop=False,
             )
 
-        def load_words(eng, name, src):
-            t = sb.tile([P, src.shape[1]], U8, name=name, align_bytes=64)
-            eng.dma_start(out=t[:].bitcast(I32), in_=src.bitcast(I32))
-            return t
+        def xq_wc_pass(i):
+            nc.tensor.matmul_mx(
+                out=z[i][:], lhsT=xq[:, span(i, P * E2M1_BYTES)].bitcast(E2M1), lhsT_scale=xq_plane[:, span(i, P)],
+                rhs=wc.bitcast(E4M3), rhs_scale=wc_plane[:], start=False, stop=True,
+            )
 
-        def fp8(w, z):
-            return w[z].rearrange("p n j -> p (n j)")
 
-        ident = sb.tile([P, P], F32, name="ident")
-        make_identity(nc, ident[:])
-        xt_s = plane("xt_s", 2, nc.vector)
-        wa_s = plane("wa_s", 2, nc.vector)
-        wc_s = plane("wc_s", 1, nc.vector)
-        xq_s = plane("xq_s", 1, nc.vector)
-        wy_s = plane("wy_s", 2, nc.vector)
-        wb_s = plane("wb_s", 1, nc.vector)
-        warm = sb.tile([P, 1], F32, name="warm")
-        nc.vector.memset(warm[:], 1.0)
+        partial = {}
+        rstd = {}
+        levelled = {}
 
-        for r in range(4):
-            load_scale_row(nc.sync, xt_s, xt_scales, r)
-            load_scale_row(nc.scalar, wa_s, wa_scales, r)
-        warm2 = sb.tile([P, 1], F32, name="warm2")
-        nc.scalar.activation(out=warm2[:], in_=warm[:], func=ACT.Abs_reciprocal_sqrt, bias=EPS)
-        fr_col = sb.tile([P, 4], F32, name="fr_col")
-        nc.sync.dma_start(out=fr_col[:], in_=fr.rearrange("(p j) o -> p (j o)", j=4))
-        xt = []
-        wa = []
-        for g in range(2):
-            xt.append(load_words(nc.sync, "xt%d" % g, fp8(xt_words, g)))
-            wa.append(load_words(nc.sync, "wa%d" % g, wa_words[g]))
-        xq = load_words(nc.sync, "xq", xq_words[0])
-        wc = load_words(nc.sync, "wc", fp8(wc_words, 0))
-        for r in range(4):
-            load_scale_row(nc.sync, xq_s, xq_scales, r)
-        for r in range(4):
-            load_scale_row(nc.gpsimd, wc_s, wc_scales, r)
-        wy = [load_words(nc.sync, "wy%d" % z, fp8(wy_words, z)) for z in range(2)]
-        for r in range(4):
-            load_scale_row(nc.sync, wy_s, wy_scales, r)
-        wb = load_words(nc.sync, "wb", wb_words[0])
-        for r in range(4):
-            load_scale_row(nc.gpsimd, wb_s, wb_scales, r)
+        def gather_statistics(i):
+            partial[i] = sb.tile([P, 6], F32, name="partial%d" % i)
+            nc.vector.bn_stats(out=partial[i][:], in_=z[i][:])
 
-        fr_ps = ps.tile([P, 4, P], F32, name="fr_ps", tag="o3")
-        for j in range(4):
-            nc.tensor.transpose(fr_ps[:, j, :], fr_col[:, j:j + 1].to_broadcast([P, P]), ident[:])
-        fr_row = sb.tile([P, W], F32, name="fr_row")
-        nc.vector.tensor_copy(out=fr_row[:].rearrange("m (p j) -> m p j", j=4), in_=fr_ps[:].rearrange("m j p -> m p j"))
-
-        z = [ps.tile([P, W], F32, name="z%d" % i, tag="z%d" % i) for i in range(TILES)]
-        stats = [None] * TILES
-        mv = [None] * TILES
-        rstd = [None] * TILES
-        cen = [None] * TILES
-        hid = [None] * TILES
-        turned = [None] * TILES
-        grouped = [None] * TILES
-        codes = [None] * TILES
-        hsc = [None] * TILES
-
-        def cols(i, width=1):
-            return slice(i * P * width, (i + 1) * P * width)
-
-        def first_layer(i, g):
-            if g < 2:
-                nc.tensor.matmul_mx(
-                    out=z[i][:], lhsT=xt[g][:, cols(i, 4)].bitcast(E4M3), lhsT_scale=xt_s[:, g * W + i * P:g * W + (i + 1) * P],
-                    rhs=wa[g][:].bitcast(E2M1), rhs_scale=wa_s[:, g * W:(g + 1) * W], start=(g == 0), stop=False)
-            else:
-                nc.tensor.matmul_mx(
-                    out=z[i][:], lhsT=xq[:, cols(i, 2)].bitcast(E2M1), lhsT_scale=xq_s[:, cols(i)],
-                    rhs=wc[:].bitcast(E4M3), rhs_scale=wc_s[:], start=False, stop=True)
-
-        def row_stats(i):
-            stats[i] = sb.tile([P, 6], F32, name="stats%d" % i)
-            mv[i] = sb.tile([P, 2], F32, name="mv%d" % i)
+        def finish_statistics(i):
+            nc.vector.bn_aggr(out=moments[i][:, 1:3], in_=partial[i][:])
             rstd[i] = sb.tile([P, 1], F32, name="rstd%d" % i)
-            nc.vector.bn_stats(out=stats[i][:], in_=z[i][:])
-            nc.vector.bn_aggr(out=mv[i][:], in_=stats[i][:])
-            nc.scalar.activation(out=rstd[i][:], in_=mv[i][:, 1:2], func=ACT.Abs_reciprocal_sqrt, bias=EPS)
-
-        def centre(i):
-            cen[i] = sb.tile([P, W], F32, name="cen%d" % i)
-            nc.vector.scalar_tensor_tensor(out=cen[i][:], in0=z[i][:], scalar=mv[i][:, 0:1], in1=fr_row[:],
-                                           op0=ALU.subtract, op1=ALU.mult)
+            nc.scalar.activation(out=rstd[i][:], in_=moments[i][:, 2:3], func=ACT.Abs_reciprocal_sqrt, bias=EPS)
 
         def level(i):
-            hid[i] = sb.tile([P, W], BF16, name="hid%d" % i)
-            nc.scalar.activation(out=hid[i][:].rearrange("t (u p e) -> t u p e", u=2, e=2),
-                                 in_=cen[i][:].rearrange("t (p u e) -> t u p e", u=2, e=2),
-                                 func=ACT.Copy, scale=rstd[i][:])
+            by_slot = z[i][:].rearrange("t (p j) -> t j p", j=PACK)
+            if i == vector_tile:
+                levelled[i] = sb.tile([P, PACK, P], F32, name="levelled%d" % i)
+                nc.vector.tensor_scalar(
+                    out=levelled[i][:], in0=by_slot, scalar1=moments[i][:, 1:2], scalar2=rstd[i][:],
+                    op0=ALU.subtract, op1=ALU.mult,
+                )
+            else:
+                affine = sb.tile([P, 2], F32, name="affine%d" % i)
+                nc.scalar.activation(out=affine[:], in_=moments[i][:, 0:2], func=ACT.Copy, scale=rstd[i][:])
+                levelled[i] = sb.tile([P, PACK, P], F32, name="levelled%d" % i)
+                nc.scalar.activation(
+                    out=levelled[i][:], in_=by_slot, func=ACT.Identity, scale=affine[:, 0:1], bias=affine[:, 1:2]
+                )
+
+
+        turned = {}
+        hid_codes = {}
+        hid_plane = {}
 
         def turn(i):
-            turned[i] = ps.tile([P, 2, P], F32, name="turned%d" % i, tag="z%d" % i)
-            for u in range(2):
-                nc.tensor.transpose(turned[i][:, u, :], hid[i][:].bitcast(F32)[:, cols(u)], ident[:])
+            turned[i] = ps.tile([P, PACK, P], F32, name="turned%d" % i, tag="hidden%d" % i)
+            for j in range(PACK):
+                nc.tensor.transpose(turned[i][:, j, :], levelled[i][:, j, :], identity[:])
 
-        def gather(i):
-            grouped[i] = sb.tile([P, W], BF16, name="grouped%d" % i, align_bytes=64)
-            nc.scalar.copy(out=grouped[i][:].bitcast(F32).rearrange("p (t u) -> p t u", u=2),
-                           in_=turned[i][:].rearrange("p u t -> p t u"))
+        def weigh_and_quantise(i):
+            factor = fr_pos if i == vector_tile else fr_neg
+            hid = sb.tile([P, P, PACK], BF16, name="hid%d" % i, align_bytes=64)
+            nc.vector.tensor_tensor(
+                out=hid[:], in0=turned[i][:].rearrange("p j t -> p t j"),
+                in1=factor[:].unsqueeze(1).to_broadcast([P, P, PACK]), op=ALU.mult,
+            )
+            hid_codes[i] = sb.tile([P, P], U32, name="hid_codes%d" % i, align_bytes=64)
+            hid_plane[i] = sb.tile([P, P], U8, name="hid_plane%d" % i, align_bytes=64)
+            nc.vector.quantize_mx(
+                out=hid_codes[i][:].bitcast(E4M3), scales=hid_plane[i][:], in_=hid[:].rearrange("p t j -> p (t j)")
+            )
 
-        def quantise(i):
-            codes[i] = sb.tile([P, P], U32, name="codes%d" % i, align_bytes=64)
-            hsc[i] = sb.tile([P, P], U8, name="hsc%d" % i, align_bytes=64)
-            nc.vector.quantize_mx(out=codes[i][:].bitcast(E4M3), scales=hsc[i][:], in_=grouped[i][:])
 
-        banks = [(0, 256, 0, 2, "o0"), (0, 256, 2, 2, "o1"), (256, 128, 0, 4, "o2"), (384, 128, 0, 2, "o3"), (384, 128, 2, 2, "z0")]
-        y = [None] * len(banks)
+        sums = {}
+        closes_bank = set()
 
-        def skip(b):
-            t0, nt, a0, na, tag = banks[b]
-            y[b] = ps.tile([P, na, nt], F32, name="y%d" % b, tag=tag)
-            for a in range(a0, a0 + na):
-                for g in range(2):
+        def skip(i, feature_tiles, tag):
+            bank = ps.tile([P, len(feature_tiles), P], F32, name="sums%d_%d" % (i, feature_tiles[0]), tag=tag)
+            closes_bank.add((i, feature_tiles[-1]))
+            for slot, a in enumerate(feature_tiles):
+                sums[i, a] = (bank, slot)
+                for g in range(K_PASSES):
+                    codes, scales = xt_tile(i, g)
                     nc.tensor.matmul_mx(
-                        out=y[b][:, a - a0, :], lhsT=wy[g][:, cols(a, 4)].bitcast(E4M3),
-                        lhsT_scale=wy_s[:, g * W + a * P:g * W + (a + 1) * P],
-                        rhs=xt[g][:, 4 * t0:4 * (t0 + nt)].bitcast(E4M3), rhs_scale=xt_s[:, g * W + t0:g * W + t0 + nt],
-                        start=(a == a0 and g == 0), stop=False)
+                        out=bank[:, slot, :], lhsT=wy[g][:, span(a, P * E4M3_BYTES)].bitcast(E4M3),
+                        lhsT_scale=wy_plane[:, span(g * FEATURE_TILES + a, P)],
+                        rhs=codes, rhs_scale=scales, start=(slot == 0 and g == 0), stop=False,
+                    )
 
         def second_layer(i):
-            for b, (t0, nt, a0, na, tag) in enumerate(banks):
-                if t0 <= i * P < t0 + nt:
-                    for a in range(a0, a0 + na):
-                        nc.tensor.matmul_mx(
-                            out=y[b][:, a - a0, i * P - t0:(i + 1) * P - t0], lhsT=wb[:, cols(a, 2)].bitcast(E2M1),
-                            lhsT_scale=wb_s[:, cols(a)], rhs=codes[i][:].bitcast(E4M3), rhs_scale=hsc[i][:],
-                            start=False, stop=(a == a0 + na - 1 and (i + 1) * P == t0 + nt))
+            for a in range(FEATURE_TILES):
+                bank, slot = sums[i, a]
+                nc.tensor.matmul_mx(
+                    out=bank[:, slot, :], lhsT=wb[:, span(a, P * E2M1_BYTES)].bitcast(E2M1),
+                    lhsT_scale=wb_plane[:, span(a, P)], rhs=hid_codes[i][:].bitcast(E4M3), rhs_scale=hid_plane[i][:],
+                    start=False, stop=((i, a) in closes_bank),
+                )
 
-        def store(b, eng, queue):
-            t0, nt, a0, na, tag = banks[b]
-            res = sb.tile([P, na, nt], F32, name="res%d" % b)
-            if eng == "s":
-                nc.scalar.copy(out=res[:], in_=y[b][:])
-            else:
-                nc.vector.tensor_copy(out=res[:], in_=y[b][:])
-            queue.dma_start(out=out.rearrange("(a p) t -> p a t", p=P)[:, a0:a0 + na, t0:t0 + nt], in_=res[:])
+        out_by_tile = out.rearrange("(a p) t -> p a t", p=P)
 
-        for i, g in [(0, 0), (1, 0), (0, 1), (0, 2), (1, 1), (1, 2)]:
-            first_layer(i, g)
-        for i in range(2, 4):
-            for g in range(3):
-                first_layer(i, g)
-        row_stats(0)
-        centre(0)
+        def store_pair(i, a, copy, queue):
+            bank, slot = sums[i, a]
+            result = sb.tile([P, 2, P], F32, name="result%d_%d" % (i, a))
+            copy(out=result[:], in_=bank[:, slot:slot + 2, :])
+            queue.dma_start(out=out_by_tile[:, a:a + 2, span(i, P)], in_=result[:])
+
+        def store(i):
+            for a in (0, 2):
+                store_pair(i, a, nc.scalar.copy, nc.sync)
+
+
+        xt_wa_pass(0, 0)
+        xt_wa_pass(0, 1)
+        xt_wa_pass(1, 0)
+        xq_wc_pass(0)
+        xt_wa_pass(1, 1)
+        xq_wc_pass(1)
+        for i in range(2, TILES):
+            for g in range(K_PASSES):
+                xt_wa_pass(i, g)
+            xq_wc_pass(i)
+
+        gather_statistics(0)
+        finish_statistics(0)
         level(0)
-        turn(0)
-        row_stats(1)
-        centre(1)
-        level(1)
-        gather(0)
-        skip(0)
-        skip(1)
-        turn(1)
-        row_stats(2)
-        quantise(0)
-        centre(2)
+        gather_statistics(1)
+        gather_statistics(2)
+        finish_statistics(1)
+        finish_statistics(2)
         level(2)
-        gather(1)
-        second_layer(0)
-        skip(2)
-        turn(2)
-        row_stats(3)
-        quantise(1)
-        centre(3)
+        gather_statistics(3)
+        level(1)
+        finish_statistics(3)
         level(3)
-        gather(2)
-        second_layer(1)
+
+        all_features = list(range(FEATURE_TILES))
+        skip(0, all_features, "sums0")
+        turn(0)
+        weigh_and_quantise(0)
+        skip(1, all_features, "sums1")
+        turn(1)
+        turn(2)
+        weigh_and_quantise(1)
+        skip(2, all_features, "sums2")
+        second_layer(0)
+        store(0)
         turn(3)
-        gather(3)
-        store(0, "v", nc.sync)
-        quantise(2)
-        quantise(3)
-        skip(3)
-        skip(4)
+        weigh_and_quantise(2)
+        second_layer(1)
+        store(1)
+        skip(3, all_features[:2], "sums3")
+        weigh_and_quantise(3)
         second_layer(2)
+        store(2)
+        skip(3, all_features[2:], "hidden0")
         second_layer(3)
-        store(1, "s", nc.sync)
-        store(2, "v", nc.sync)
-        store(4, "s", nc.scalar)
-        store(3, "v", nc.sync)
+        store_pair(3, 0, nc.vector.tensor_copy, nc.sync)
+        store_pair(3, 2, nc.scalar.copy, nc.scalar)

from contextlib import ExitStack

import concourse.mybir as mybir
from concourse.masks import make_identity

K, L, T, R, N = 1024, 512, 512, 512, 512
FLOPS = 2 * T * R * (K + L) + 2 * N * T * (R + K)

F32 = mybir.dt.float32
BF16 = mybir.dt.bfloat16
I32 = mybir.dt.int32
U32 = mybir.dt.uint32
U8 = mybir.dt.uint8
E4M3 = mybir.dt.float8_e4m3fn_x4
E2M1 = mybir.dt.float4_e2m1fn_x4
ACT = mybir.ActivationFunctionType
ALU = mybir.AluOpType

P = 128
PACK = 4
COLS = 512
TILES = T // P
FEATURE_TILES = N // P
K_PASSES = K // (P * PACK)
E4M3_BYTES = 4
E2M1_BYTES = 2
QUADRANT = 32
EPS = 0.01


def span(i, width):
    return slice(i * width, (i + 1) * width)


def tile_mix_hidden_rows_levelled_kernel(
    tc, xt_words, xt_scales, wa_words, wa_scales, xq_words, xq_scales, wc_words, wc_scales,
    fr, wb_words, wb_scales, wy_words, wy_scales, out,
):
    nc = tc.nc
    with ExitStack() as ctx:
        sb = ctx.enter_context(tc.tile_pool(name="sb", bufs=1))
        ps = ctx.enter_context(tc.psum_pool(name="ps", bufs=1))
        ctx.enter_context(tc.manual_schedule())


        def zeroed_plane(name, passes, engine):
            plane = sb.tile([P, passes * COLS], U8, name=name, align_bytes=64)
            engine.memset(plane[:].bitcast(I32), 0)
            return plane

        def load_scale_rows(queue, plane, scales, rows):
            passes = scales.shape[0]
            by_r = scales.bitcast(I32).rearrange("g (q r) c -> r q g c", r=4)
            for r in rows:
                queue.dma_start(
                    out=plane[r:P:QUADRANT, :].bitcast(I32).rearrange("q (g c) -> q g c", g=passes), in_=by_r[r]
                )

        def load_words(name, words):
            passes, width = words.shape[0], words.shape[2]
            packed = sb.tile([P, passes * width], U8, name=name, align_bytes=64)
            nc.sync.dma_start(
                out=packed[:].bitcast(I32).rearrange("p (g c) -> p g c", g=passes),
                in_=words.bitcast(I32).rearrange("g p c -> p g c"),
            )
            return [packed[:, span(g, width)] for g in range(passes)]

        def merged(words):
            return words.rearrange("g p c j -> g p (c j)")

        xt_plane = zeroed_plane("xt_plane", K_PASSES, nc.gpsimd)
        wa_plane = zeroed_plane("wa_plane", K_PASSES, nc.vector)
        wc_plane = zeroed_plane("wc_plane", 1, nc.vector)
        xq_plane = zeroed_plane("xq_plane", 1, nc.vector)
        wy_plane = zeroed_plane("wy_plane", K_PASSES, nc.vector)
        wb_plane = zeroed_plane("wb_plane", 1, nc.vector)

        vector_tile = 1
        moments = [sb.tile([P, 3], F32, name="moments%d" % i) for i in range(TILES)]
        for i in range(TILES):
            if i != vector_tile:
                nc.vector.memset(moments[i][:, 0:1], -1.0)

        half_bytes = 2 * P * E4M3_BYTES
        wa = load_words("wa", wa_words)
        load_scale_rows(nc.scalar, xt_plane, xt_scales, range(4))
        table_preload = sb.tile([P, 1], F32, name="table_preload")
        nc.scalar.activation(out=table_preload[:], in_=moments[0][:, 0:1], func=ACT.Abs_reciprocal_sqrt, bias=EPS)
        load_scale_rows(nc.sync, wa_plane, wa_scales, (0, 1))
        xt_halves = [load_words("xt_half0", merged(xt_words)[:, :, span(0, half_bytes)])]
        load_scale_rows(nc.sync, wa_plane, wa_scales, (2, 3))
        load_scale_rows(nc.sync, xq_plane, xq_scales, (0,))
        wc = load_words("wc", merged(wc_words))[0]
        load_scale_rows(nc.sync, xq_plane, xq_scales, (1, 2, 3))
        xq = load_words("xq", xq_words)[0]
        load_scale_rows(nc.sync, wc_plane, wc_scales, (0, 1))
        load_scale_rows(nc.gpsimd, wc_plane, wc_scales, (2, 3))
        xt_halves.append(load_words("xt_half1", merged(xt_words)[:, :, span(1, half_bytes)]))
        wy = load_words("wy", merged(wy_words))
        load_scale_rows(nc.sync, wy_plane, wy_scales, range(4))
        wb = load_words("wb", wb_words)[0]
        load_scale_rows(nc.sync, wb_plane, wb_scales, range(4))

        identity = sb.tile([P, P], F32, name="identity")
        make_identity(nc, identity[:])
        fr_pos = sb.tile([P, PACK], F32, name="fr_pos")
        nc.gpsimd.dma_start(out=fr_pos[:], in_=fr.rearrange("(p j) o -> p (j o)", j=PACK))
        fr_neg = sb.tile([P, PACK], F32, name="fr_neg")
        nc.gpsimd.tensor_scalar(out=fr_neg[:], in0=fr_pos[:], scalar1=-1.0, scalar2=0.0, op0=ALU.mult, op1=ALU.add)

        def xt_tile(i, g):
            codes = xt_halves[i // 2][g][:, span(i % 2, P * E4M3_BYTES)].bitcast(E4M3)
            return codes, xt_plane[:, span(g * TILES + i, P)]


        z = [ps.tile([P, R], F32, name="z%d" % i, tag="hidden%d" % i) for i in range(TILES)]

        def xt_wa_pass(i, g):
            codes, scales = xt_tile(i, g)
            nc.tensor.matmul_mx(
                out=z[i][:], lhsT=codes, lhsT_scale=scales,
                rhs=wa[g].bitcast(E2M1), rhs_scale=wa_plane[:, span(g, COLS)], start=(g == 0), stop=False,
            )

        def xq_wc_pass(i):
            nc.tensor.matmul_mx(
                out=z[i][:], lhsT=xq[:, span(i, P * E2M1_BYTES)].bitcast(E2M1), lhsT_scale=xq_plane[:, span(i, P)],
                rhs=wc.bitcast(E4M3), rhs_scale=wc_plane[:], start=False, stop=True,
            )


        partial = {}
        rstd = {}
        levelled = {}

        def gather_statistics(i):
            partial[i] = sb.tile([P, 6], F32, name="partial%d" % i)
            nc.vector.bn_stats(out=partial[i][:], in_=z[i][:])

        def finish_statistics(i):
            nc.vector.bn_aggr(out=moments[i][:, 1:3], in_=partial[i][:])
            rstd[i] = sb.tile([P, 1], F32, name="rstd%d" % i)
            nc.scalar.activation(out=rstd[i][:], in_=moments[i][:, 2:3], func=ACT.Abs_reciprocal_sqrt, bias=EPS)

        def level(i):
            by_slot = z[i][:].rearrange("t (p j) -> t j p", j=PACK)
            if i == vector_tile:
                levelled[i] = sb.tile([P, PACK, P], F32, name="levelled%d" % i)
                nc.vector.tensor_scalar(
                    out=levelled[i][:], in0=by_slot, scalar1=moments[i][:, 1:2], scalar2=rstd[i][:],
                    op0=ALU.subtract, op1=ALU.mult,
                )
            else:
                affine = sb.tile([P, 2], F32, name="affine%d" % i)
                nc.scalar.activation(out=affine[:], in_=moments[i][:, 0:2], func=ACT.Copy, scale=rstd[i][:])
                levelled[i] = sb.tile([P, PACK, P], F32, name="levelled%d" % i)
                nc.scalar.activation(
                    out=levelled[i][:], in_=by_slot, func=ACT.Identity, scale=affine[:, 0:1], bias=affine[:, 1:2]
                )


        turned = {}
        hid_codes = {}
        hid_plane = {}

        def turn(i):
            turned[i] = ps.tile([P, PACK, P], F32, name="turned%d" % i, tag="hidden%d" % i)
            for j in range(PACK):
                nc.tensor.transpose(turned[i][:, j, :], levelled[i][:, j, :], identity[:])

        def weigh_and_quantise(i):
            factor = fr_pos if i == vector_tile else fr_neg
            hid = sb.tile([P, P, PACK], BF16, name="hid%d" % i, align_bytes=64)
            nc.vector.tensor_tensor(
                out=hid[:], in0=turned[i][:].rearrange("p j t -> p t j"),
                in1=factor[:].unsqueeze(1).to_broadcast([P, P, PACK]), op=ALU.mult,
            )
            hid_codes[i] = sb.tile([P, P], U32, name="hid_codes%d" % i, align_bytes=64)
            hid_plane[i] = sb.tile([P, P], U8, name="hid_plane%d" % i, align_bytes=64)
            nc.vector.quantize_mx(
                out=hid_codes[i][:].bitcast(E4M3), scales=hid_plane[i][:], in_=hid[:].rearrange("p t j -> p (t j)")
            )


        sums = {}
        closes_bank = set()

        def skip(i, feature_tiles, tag):
            bank = ps.tile([P, len(feature_tiles), P], F32, name="sums%d_%d" % (i, feature_tiles[0]), tag=tag)
            closes_bank.add((i, feature_tiles[-1]))
            for slot, a in enumerate(feature_tiles):
                sums[i, a] = (bank, slot)
                for g in range(K_PASSES):
                    codes, scales = xt_tile(i, g)
                    nc.tensor.matmul_mx(
                        out=bank[:, slot, :], lhsT=wy[g][:, span(a, P * E4M3_BYTES)].bitcast(E4M3),
                        lhsT_scale=wy_plane[:, span(g * FEATURE_TILES + a, P)],
                        rhs=codes, rhs_scale=scales, start=(slot == 0 and g == 0), stop=False,
                    )

        def second_layer(i):
            for a in range(FEATURE_TILES):
                bank, slot = sums[i, a]
                nc.tensor.matmul_mx(
                    out=bank[:, slot, :], lhsT=wb[:, span(a, P * E2M1_BYTES)].bitcast(E2M1),
                    lhsT_scale=wb_plane[:, span(a, P)], rhs=hid_codes[i][:].bitcast(E4M3), rhs_scale=hid_plane[i][:],
                    start=False, stop=((i, a) in closes_bank),
                )

        out_by_tile = out.rearrange("(a p) t -> p a t", p=P)

        def store_pair(i, a, copy, queue):
            bank, slot = sums[i, a]
            result = sb.tile([P, 2, P], F32, name="result%d_%d" % (i, a))
            copy(out=result[:], in_=bank[:, slot:slot + 2, :])
            queue.dma_start(out=out_by_tile[:, a:a + 2, span(i, P)], in_=result[:])

        def store(i):
            for a in (0, 2):
                store_pair(i, a, nc.scalar.copy, nc.sync)


        xt_wa_pass(0, 0)
        xt_wa_pass(0, 1)
        xt_wa_pass(1, 0)
        xq_wc_pass(0)
        xt_wa_pass(1, 1)
        xq_wc_pass(1)
        for i in range(2, TILES):
            for g in range(K_PASSES):
                xt_wa_pass(i, g)
            xq_wc_pass(i)

        gather_statistics(0)
        finish_statistics(0)
        level(0)
        gather_statistics(1)
        gather_statistics(2)
        finish_statistics(1)
        finish_statistics(2)
        level(2)
        gather_statistics(3)
        level(1)
        finish_statistics(3)
        level(3)

        all_features = list(range(FEATURE_TILES))
        skip(0, all_features, "sums0")
        turn(0)
        weigh_and_quantise(0)
        skip(1, all_features, "sums1")
        turn(1)
        turn(2)
        weigh_and_quantise(1)
        skip(2, all_features, "sums2")
        second_layer(0)
        store(0)
        turn(3)
        weigh_and_quantise(2)
        second_layer(1)
        store(1)
        skip(3, all_features[:2], "sums3")
        weigh_and_quantise(3)
        second_layer(2)
        store(2)
        skip(3, all_features[2:], "hidden0")
        second_layer(3)
        store_pair(3, 0, nc.vector.tensor_copy, nc.sync)
        store_pair(3, 2, nc.scalar.copy, nc.scalar)
